import numpy as np, ml_dtypes
CORES = [5,29,101,125,133,157,229,253]
N = 8
import mx_ref
BF = ml_dtypes.bfloat16
def gentries(a):
    return np.ascontiguousarray(a.reshape(8, 16, -1).transpose(0, 2, 1)).reshape(8, -1)
def gtable(e):
    e = np.asarray(e); return np.ascontiguousarray(e.reshape(8, -1, 16).transpose(0, 2, 1)).reshape(128, -1).astype(np.int32)
def gcols(t, e):
    v = np.concatenate([t.reshape(8, 16, -1, 4), np.zeros((8, 16, 1, 4), BF)], axis=2)
    return np.ascontiguousarray(np.stack([v[g][:, e[g]] for g in range(8)])).reshape(128, -1)
def tile(rs):
    return np.stack(rs, axis=2).reshape(128, -1).astype(BF)
def pick(q, e):
    c = np.concatenate([q[0].reshape(128, -1, 4), np.zeros((128, 1, 4), np.uint8)], axis=1); s = np.concatenate([q[1], np.ones((16, 1), np.uint8)], axis=1)
    return (np.ascontiguousarray(c[:, e].reshape(128, -1)), np.ascontiguousarray(s[:, e]))
def join(*qs):
    return (np.concatenate([q[0] for q in qs], axis=1), np.concatenate([q[1] for q in qs], axis=1))
def put(q, e, v):
    c, s = q[0].reshape(128, -1, 4).copy(), q[1].copy(); c[:, e] = v[0].reshape(128, -1, 4); s[:, e] = v[1]
    return (c.reshape(128, -1), s)
def pk(c, s):
    return (np.ascontiguousarray(c), mx_ref.live(s))
def emit(q):
    return q[0], q[1]
def packed(v, rng):
    q = [mx_ref.quantize(np.ascontiguousarray(v[r])) for r in range(N)]
    return np.stack([a for a, b in q]), np.stack([mx_ref.plane(b, rng) for a, b in q])
def values_of_codes():
    e, c = np.zeros((128, 128, 4), np.float32), np.zeros((128, 2, 4), np.uint8)
    e[np.arange(128), np.arange(128), 0] = 1
    c[:127, :, 0] = np.arange(256).reshape(2, 128).T[:127]
    return mx_ref.matmul(mx_ref.quantize(e.reshape(128, 512).astype(BF)), (c.reshape(128, 8), np.full((16, 2), 127, np.uint8))).T.reshape(-1).astype(np.float64)
CODE_VALUE, SCALE_VALUE = values_of_codes(), 2.0 ** (np.arange(256) - 127.0)
def decode(q):
    return (CODE_VALUE[q[0]].reshape(16, 8, -1, 4) * SCALE_VALUE[q[1]][:, None, :, None] + 0.0).reshape(128, -1).astype(np.float32)
def f(rng, *shape):
    return mx_ref.flush((rng.standard_normal(shape, dtype=np.float32) * np.exp2(rng.integers(-2, 3, shape[:-1] + (1,)))).astype(BF))
def wide(rng, *shape, cols=0):
    v = rng.standard_normal(shape, dtype=np.float32) * np.exp2(rng.integers(-12, 13, shape)).astype(np.float32)
    if cols: v *= np.repeat(np.exp2(rng.integers(-cols, cols + 1, shape[:-2] + (1, shape[-1] // 4))) * (rng.random(shape[:-2] + (1, shape[-1] // 4)) > 0.0625), 4, axis=-1).astype(np.float32)
    return mx_ref.flush(v.astype(BF))
C, M, R = 320, 160, 3
SH = (N, 8, 2, C, 4)
def numbers_of(rng):
    return {"x": np.array(f(rng, N, 128, 4 * C)), "u": np.array(f(rng, N, 128, 512)), "v": np.array(f(rng, N, 128, 512))}
def lists_of(e, c, a):
    return {"al": np.stack([gtable(e[r]) for r in range(N)]), "nx": np.stack([gtable((512 * c + a)[r].reshape(8, 8 * C)) for r in range(N)])}
def lists(rng):
    return lists_of(rng.integers(0, C, (N, 8, C)), rng.integers(0, 5, SH), rng.integers(0, C, SH))
def layers(rng, still=0):
    w = np.array(f(rng, N, 128, 2048)).reshape(N, 8, 16, 4, 8, 16, 4)
    w[:, :, :still] = 0
    w[:, :, :, :, :, :still] = 0
    return w
def weights(rng, w):
    c, s = packed(np.ascontiguousarray(w).reshape(N, 128, 2048), rng)
    return {"wc": c, "ws": s}
def setup_inputs(rng):
    return {**numbers_of(rng), **lists(rng), **weights(rng, layers(rng))}
def setup_inputs_near(rng):
    d = numbers_of(rng)
    x = d["x"].reshape(N, 8, 16, C, 4)
    u = d["u"].reshape(N, 128, 128, 4)
    o = rng.permutation(N) % 2
    x[:, :, :8] = 0
    u[:, :, ::16] = 0
    u[:, :, 1::16] = 0
    for r in range(N):
        k = 2.0 ** -30 if o[r] == 0 else 1.0
        s = rng.integers(-1, 2, (8, 2, C)) * k
        for g in rng.permutation(8)[:4]: s[g, :, rng.integers(C)] = 2.0 ** 14 * rng.choice([-1.0, 1.0], 2)
        x[r, :, :2, :, 0] = s.astype(np.float32).astype(BF)
        t = np.where(s[:, 0] == 0, rng.integers(-1, 2, (8, C)), 0) * k
        x[r, :, 2, :, 0] = (1.125 * t).astype(np.float32).astype(BF)
        x[r, :, 3, :, 0] = (-t).astype(np.float32).astype(BF)
        for h in [0, 16, 32, 48, 64, 80, 96, 112, 1, 17]:
            u[r, h, h, 0] = k
            u[r, h - h % 16 + 2, h, 0] = 1.125 * k
            u[r, h - h % 16 + 3, h, 0] = 1.25 * k
    return {"x": x.reshape(N, 128, 4 * C), "u": u.reshape(N, 128, 512), "v": d["v"], **lists(rng), **weights(rng, layers(rng, 8))}
def setup_inputs_chain(rng):
    d = numbers_of(rng)
    e = rng.permutation(N)
    c = rng.integers(0, 5, SH)
    i = np.arange(4)
    c[e[0]] = rng.integers(1, 5, SH[1:])
    c[e[1]] = 0
    c[e[2]] = np.where(np.arange(8)[:, None] <= 2 * i, i + 1, 0)[:, None, None, :]
    c[e[3]][:, 0] = 0
    c[e[3]][:, 1] = rng.integers(1, 5, (8, C, 4))
    return {**d, **lists_of(rng.integers(0, C, (N, 8, C)), c, rng.integers(0, C, SH)), **weights(rng, layers(rng))}
def setup_inputs_twice(rng):
    d = numbers_of(rng)
    s = 2.0 ** -rng.integers(8, 15, (N, 16, C, 32)) * (1.125 + 0.25 * rng.integers(0, 4, (N, 16, C, 32)))
    s[:, :, :, 4] = 2.0 ** -rng.integers(8, 12, (N, 16, C)) * (1.125 + 0.25 * rng.integers(0, 4, (N, 16, C)))
    np.put_along_axis(s, rng.integers(8, 32, (N, 16, C, 1)), 1.96875, axis=3)
    s = s * rng.choice([-1.0, 1.0], s.shape)
    s[:, :, :, 0] = 0.125 * s[:, :, :, 4]
    s = s * np.exp2(rng.integers(10, 13, (N, 16, C, 1)))
    x = np.ascontiguousarray(s.reshape(N, 16, C, 8, 4).transpose(0, 1, 3, 2, 4)).reshape(N, 128, 4 * C)
    u = d["u"].reshape(N, 128, 128, 4)
    u[:, :, ::16] = 0
    for h in range(0, 128, 16):
        u[:, h, h, 0] = 1.0
        u[:, h + 1, h, 0] = -0.125
    w = np.array(mx_ref.flush((layers(rng).astype(np.float32) * np.float32(2.0 ** -12)).astype(BF))).reshape(N, 128, 4, 128, 4)
    i = np.arange(128)
    for b in range(4): w[:, i, b, i, b] = -1.0
    return {"x": x.astype(np.float32).astype(BF), "u": u.reshape(N, 128, 512), "v": d["v"], **lists(rng), **weights(rng, w)}
def setup_inputs_ends(rng):
    d = numbers_of(rng)
    e = rng.permutation(N)
    x = d["x"].reshape(N, 8, 16, C, 4)
    u = d["u"].reshape(N, 128, 128, 4)
    v = d["v"].reshape(N, 128, 128, 4)
    t = np.clip(rng.integers(-C, 2 * C, (N, 8, C)), 0, C - 1)
    c = 4 * rng.integers(0, 2, SH)
    a = np.clip(rng.integers(-C, 2 * C, SH), 0, C - 1)
    t[e[0]], c[e[0]], a[e[0]] = C - 1, 4, C - 1
    t[e[1]], c[e[1]], a[e[1]] = 0, 0, 0
    u[:, :, ::16] = 0
    u[:, :, 1::16] = 0
    for i in range(N):
        r = e[i]
        s = rng.integers(-1, 2, (8, C)) * 1.0
        s[rng.permutation(8)[:2]] = rng.choice([-1.0, 1.0], (2, 1))
        s = s * (2.0 ** -30 if i % 2 else 2.0 ** 14)
        x[r, :, :8] = s[:, None, :, None].astype(np.float32).astype(BF)
        for h in [0, 16, 32, 48, 64, 80, 96, 112, 1, 17]: u[r, h - h % 16:h - h % 16 + 8, h] = 2.0 ** -30 if i % 2 else 2.0 ** 30
    x[e[0]] = (2.0 ** 14 * rng.choice([-1.0, 1.0], (C, 1))).astype(np.float32).astype(BF)
    u[e[0]] = (2.0 ** 30 * rng.choice([-1.0, 1.0], (128, 1))).astype(np.float32).astype(BF)
    v[e[0]] = (2.0 ** 30 * rng.choice([-1.0, 1.0], (128, 1))).astype(np.float32).astype(BF)
    w = layers(rng, 8)
    w[e[0]][:, 8:, :, :, 8:] = 8
    w[e[1]] = 0
    v = (np.where(v < 0, -1.0, 1.0) * np.where(rng.permutation(N) % 2, 2.0 ** -30, 2.0 ** 30)[:, None, None, None]).astype(np.float32).astype(BF)
    return {"x": x.reshape(N, 128, 4 * C), "u": u.reshape(N, 128, 512), "v": v.reshape(N, 128, 512), **lists_of(t, c, a), **weights(rng, w)}
def setup_inputs_spread(rng):
    d = setup_inputs(rng)
    d["x"] = mx_ref.flush((wide(rng, N, 128, 4 * C, cols=6).astype(np.float32) * np.float32(2.0 ** -7)).astype(BF))
    return d
def check_inputs(d):
    b = []
    for k, most in (("x", 2.0 ** 14), ("u", 2.0 ** 30), ("v", 2.0 ** 30)):
        a = np.abs(d[k].astype(np.float32))
        if not (np.isfinite(a).all() and ((a == 0) | (a >= 2.0 ** -30) & (a <= most)).all()): b.append("a value of " + k)
    if not ((d["al"] >= 0) & (d["al"] < C)).all(): b.append("an entry of al")
    if not ((d["nx"] >= 0) & (d["nx"] < 2560) & (d["nx"] % 512 < C)).all(): b.append("an entry of nx")
    none, least, most = [emit(mx_ref.quantize(np.full((128, 16), k, np.float32).astype(BF)))[1][0, 0] for k in (0.0, 2.0 ** -30, 2.0 ** 30)]
    for r in range(N):
        if ((d["wc"][r] == 0x7F) | (d["wc"][r] == 0xFF)).any(): b.append("wc: a code that is no number")
        s = mx_ref.live(d["ws"][r])
        if ((s != none) & ((s < least) | (s > most))).any(): b.append("ws: a scale out of range")
        w = np.abs(decode(pk(d["wc"][r], d["ws"][r])).astype(np.float64)).reshape(128, 512, 4)
        if not (np.sum(w, axis=(0, 2)) <= 2048).all(): b.append("a column of W adds up to more than 2048")
    return b
def reference(x, u, v, al, nx, wc, ws):
    qu = [mx_ref.quantize(u[r]) for r in range(N)]
    lay = [pk(wc[r], ws[r]) for r in range(N)]
    now = [x[r] for r in range(N)]
    ad = np.stack([gentries(al[r]) for r in range(N)])
    follow = [gentries(nx[r]) for r in range(N)]
    for t in range(R):
        made = []
        for r in range(N):
            q = mx_ref.quantize(now[r])
            s = mx_ref.matmul(qu[r], q)
            edge = 2 * (s[1] > 0) + (s[17] > 0)
            on = np.ones(C, bool)
            for g in range(8):
                bit = s[16 * g][ad[r, g]] > 0
                n = follow[r][g][4 * C * bit + 4 * ad[r, g] + edge]
                ad[r, g] = np.where(on, n % 512, ad[r, g])
                on = on & (n >= 512)
                edge = np.where(on, n // 512 - 1, 0)
            made.append(mx_ref.quantize(gcols(decode(q).astype(BF), ad[r])))
        ad[:, :, C - M:] = np.roll(ad[:, :, C - M:], 1, axis=0)
        for r in range(N):
            q = join(pick(made[r], np.arange(C - M)), pick(made[r - 1], np.arange(C - M, C)))
            own = decode(q)
            now[r] = tile([mx_ref.matmul(pick(lay[r], np.arange(128 * b, 128 * b + 128)), q) * np.float32(0.015625) + own[:, b::4] for b in range(4)])
    y, oa = np.zeros((N, 128, C), np.float32), np.zeros((N, 8, C), np.float32)
    oc, osc = np.zeros((N, 128, 4 * C), np.uint8), np.zeros((N, 16, C), np.uint8)
    for r in range(N):
        q = mx_ref.quantize(now[r])
        y[r] = mx_ref.matmul(mx_ref.quantize(v[r]), q)
        oa[r] = ad[r]
        oc[r], osc[r] = emit(q)
    return {"y": y, "oa": oa, "oc": oc, "osc": osc}

import math
from concourse.bass import DstId, RemoteDMATransfer
from concourse.mybir import dt, AluOpType as A, AxisListType, ActivationFunctionType as AF

N, C, H, R = 8, 320, 160, 3
BF, F32, I32, U16, U8, MX = "bfloat16", "float32", "int32", "uint16", "uint8", "float8_e4m3fn_x4"
MAGIC = 12582912.0
BIG = 1.5 * 2.0 ** 32


def _scratch():
    s = {}

    def sb(name, n, t):
        s[name] = ("sbuf", [128, n], t)
    for k in range(8):
        s["pk%d" % k] = ("psum", [128, 512], F32)
    sb("ub", 512, BF); sb("uq", 128, MX); sb("up", 128, U8); sb("uq2", 128, MX); sb("up2", 128, U8)
    sb("vb", 512, BF); sb("vq", 128, MX); sb("vp", 128, U8)
    sb("wq", 512, MX); sb("wp", 512, U8)
    sb("one", 516, BF); sb("eb", 516, BF); sb("eb64", 516, BF)
    sb("ec", 512, MX); sb("es", 512, U8); sb("e64c", 512, MX); sb("e64s", 512, U8)
    sb("ci", 64, I32); sb("cf", 64, F32); sb("uls", 8, U16); sb("sg", 100, F32); sb("idl", 20, U16)
    sb("ali", 20, I32); sb("l0", 20, U16)
    sb("nt", 640, I32); sb("ni", 640, I32); sb("nf", 3840, F32); sb("tw", 640, F32)
    sb("iw", 320, F32); sb("orow", 320, F32); sb("yb", 320, F32); sb("kx", 120 * R, F32); sb("hb", 100 * R, I32)
    for r in range(R + 1):
        sb("x%d" % r, 1280, BF); sb("qx%d" % r, 320, MX); sb("sx%d" % r, 320, U8)
    for r in range(R):
        sb("f%d" % r, 1280, BF); sb("fp%d" % r, 1280, BF); sb("z%d" % r, 1280, BF)
        sb("qz%d" % r, 320, MX); sb("sz%d" % r, 320, U8)
        sb("qp%d" % r, 320, MX); sb("sp%d" % r, 320, U8)
        sb("rq%d" % r, 320, MX); sb("rs%d" % r, 320, U8)
        sb("ll%d" % r, 10, U16); sb("rl%d" % r, 10, U16)
        sb("bw%d" % r, 320, BF); sb("br%d" % r, 640, BF); sb("bt%d" % r, 640, BF)
        sb("er%d" % r, 640, BF); sb("et%d" % r, 640, BF)
        sb("tr%d" % r, 640, F32); sb("gt%d" % r, 640, F32)
        sb("fs%d" % r, 1000, F32); sb("is%d" % r, 320, I32)
        sb("us%d" % r, 100, U16)
    return s


SCRATCH = _scratch()
SEMAPHORES = (["vq", "sq", "tq", "gq", "loc"]
              + ["ld_x0", "ld_x1", "ld_u", "ld_v", "ld_w", "ld_al", "ld_nx", "outs"]
              + ["kx%d" % r for r in range(R)]
              + ["%s%d%d" % (k, r, h) for k in ("rc", "rp", "qa") for r in range(R) for h in range(2)]
              + ["%s%d" % (k, r) for k in ("rl", "la") for r in range(R)])


def _relays(core, nxt, topo):
    w = [c for c in topo.cores_of(core) if c != core and topo.may_write(c, nxt)]
    near = [c for c in w if topo.die(c) == topo.die(core)]
    far = [c for c in w if topo.die(c) != topo.die(core)]
    return near[0], near[1], far[0]


def _mask(es):
    m = 0
    for e in es:
        m |= 1 << e
    return m


def _hand_on(g, core, T, topo):
    mine = [c for c in topo.cores_of(core) if T.rank_of(c) is not None]
    if not mine:
        return
    nxt = T.cores[(T.rank_of(mine[0]) + 1) % N]
    rel = _relays(mine[0], nxt, topo)
    if core not in rel:
        return
    k = rel.index(core)
    rid, pid = topo.addr(nxt, core)
    m = topo.mask(core, nxt)
    ne = len(topo.engines(core, nxt))
    near = len(topo.engines(mine[0], core))
    n = 0
    for r in range(R):
        for h in range(2):
            if k == 0:
                g.wait_ge(T.sem["rp%d%d" % (r, h)], near)
                g.remote_dma(T["sp%d" % r][:, H * h:H * h + H], T["rs%d" % r][:, H * h:H * h + H],
                             T.sem["qa%d%d" % (r, h)], T.sem.loc, pid, rid, m)
            else:
                a = H * h + 80 * (k - 1)
                g.wait_ge(T.sem["rc%d%d" % (r, h)], near // 2)
                g.remote_dma(T["qp%d" % r][:, a:a + 80].bitcast(dt.uint8), T["rq%d" % r][:, a:a + 80].bitcast(dt.uint8),
                             T.sem["qa%d%d" % (r, h)], T.sem.loc, pid, rid, m)
            n += ne
        if k == 0:
            g.wait_ge(T.sem["rl%d" % r], near)
            g.remote_dma(T["ll%d" % r][:], T["rl%d" % r][:], T.sem["la%d" % r], T.sem.loc, pid, rid, m)
            n += ne
    g.wait_ge(T.sem.loc, n)


def rank_program(g, core, T, topo):
    rank = T.rank_of(core)
    if rank is None:
        return _hand_on(g, core, T, topo)
    nxt = T.cores[(rank + 1) % N]
    rel = _relays(core, nxt, topo)
    before = T.cores[(rank - 1) % N]
    far_engines = len(topo.engines(_relays(before, core, topo)[0], core))
    Q = {"v": g.vector, "s": g.scalar, "t": g.tensor, "g": g, "y": g.sync}
    cnt = {"v": 0, "s": 0, "t": 0, "g": 0}
    seen = {k: {} for k in Q}
    dma_n = {}
    loc = [0]

    def need(e, toks):
        for t in toks:
            if isinstance(t, list):
                need(e, t)
            elif seen[e].get(t[0], 0) < t[1]:
                Q[e].wait_ge(T.sem[t[0]], t[1])
                seen[e][t[0]] = t[1]

    def op(e, toks, name, *a, **k):
        need(e, toks)
        q = Q[e]
        f = {"cp": lambda: q.tensor_copy(*a), "tt": lambda: q.tensor_tensor(*a), "ts": lambda: q.tensor_scalar(*a),
             "ms": lambda: q.memset(*a), "tp": lambda: q.transpose(*a), "qz": lambda: q.quantize_mx(*a),
             "scan": lambda: q.tensor_tensor_scan(*a), "act": lambda: q.activation(*a, **k), "mm": lambda: q.matmul_mx(*a),
             "iota": lambda: q.iota(*a, **k), "sel": lambda: q.affine_select(*a)}[name]
        f().then_inc(T.sem[e + "q"], 1)
        cnt[e] += 1
        return (e + "q", cnt[e])

    def dma(e, toks, out, in_, sem):
        need(e, toks)
        Q[e].dma_start(out, in_).then_inc(T.sem[sem], 16)
        dma_n[sem] = dma_n.get(sem, 0) + 16

    def done(sem):
        return (sem, dma_n[sem])

    banks = [T["pk%d" % k] for k in range(8)]
    readers = [[] for k in range(8)]
    turn = [0]

    def bank():
        k = turn[0] % 8
        turn[0] += 1
        return k

    def mm(toks, k, n, lc, ls, b, rc, rs, a, start=True, stop=True):
        w = [toks, readers[k]] if start else [toks]
        if start:
            readers[k] = []
        return op("t", w, "mm", banks[k][:, 0:n], lc[:, 128 * b:128 * b + 128], ls[:, 128 * b:128 * b + 128],
                  rc[:, a:a + n], rs[:, a:a + n], start, stop)

    ci, cf = T.ci, T.cf

    def icol(k):
        return ci[:, k:k + 1]

    def col(k):
        return cf[:, k:k + 1]

    gi = op("g", [], "iota", ci[:, 0:1], [[0, 1]], 0, 1)
    gn = op("g", [], "iota", T.nt[:, 320:640], [[1, 4], [4, 80]], 0, 0)
    gi3 = op("g", [], "iota", ci[:, 32:40], [[16, 8]], 0, 0)
    g_id = op("g", [], "iota", T.ni[:, 0:20], [[16, 10], [0, 2]], 0, 0)
    lanes = {"y": [], "s": []}
    for i in range(16):
        lanes["s" if i % 2 else "y"].append(i)

    def table_loads(q, t):
        for l in lanes[q]:
            if l // 8 == t:
                e = (l // 2) % 4
                dma(q, [], T.nt[l:128:16, 0:320], T.nx[e:128:4, 80 * t:80 * t + 80], "ld_nx")
                if t:
                    dma(q, [gn], T.nt[l:128:16, 320:640], T.nx[e:128:4, 0:80], "ld_nx")
    table_loads("y", 0)
    table_loads("s", 0)
    dma("s", [], T.ub[:], T.u[:], "ld_u")
    dma("y", [], T.x0[:, 0:640], T.x[:, 0:640], "ld_x0")
    table_loads("s", 1)
    table_loads("y", 1)
    dma("y", [], T.x0[:, 640:1280], T.x[:, 640:1280], "ld_x1")
    dma("s", [], T.ali[:], T.al[:], "ld_al")
    dma("y", [], T.wq[:].bitcast(dt.uint8), T.wc[:], "ld_w")
    dma("y", [], T.wp[:], T.ws[:], "ld_w")
    dma("y", [], T.vb[:], T.v[:], "ld_v")

    o1 = op("v", [gi], "ts", icol(1), icol(0), 15, None, A.bitwise_and)
    op("v", [], "ts", icol(2), icol(0), 4, 1, A.arith_shift_right, A.bitwise_and)
    op("v", [], "ts", icol(3), icol(0), 1, 3, A.arith_shift_right, A.bitwise_and)
    o4 = op("v", [], "ts", icol(4), icol(0), 1, None, A.bitwise_and)
    o5 = op("v", [o4], "cp", cf[:, 1:5], ci[:, 1:5])
    LF, GF, EF, YF = 1, 2, 3, 4
    ln2, ln16 = math.log(2.0), math.log(16.0)
    b2 = -ln2 + math.log(0.95)
    v_one = op("v", [], "ms", T.one[:], 1.0)
    op("v", [o5], "tt", col(5), col(GF), col(YF), A.max)
    op("v", [], "ts", col(6), col(EF), -1.0, 3.0, A.mult, A.add)
    k1 = op("v", [], "ts", col(14), col(YF), -1.0, 1.0, A.mult, A.add)
    k2 = op("v", [k1], "ts", col(7), col(5), 3.0, 1.0, A.mult, A.add)
    k3 = op("v", [k2], "tt", col(8), col(6), col(7), A.mult)
    q1 = op("s", [k3], "act", col(9), col(8), AF.Exp, scale=ln2)
    q2 = op("s", [q1], "act", col(10), col(9), AF.Identity, bias=MAGIC)
    op("v", [], "ts", col(12), col(GF), (ln2 - ln16) / 512.0, ln16 / 512.0, A.mult, A.add)
    c5 = op("v", [], "ts", col(13), col(GF), b2 + ln16, -ln16, A.mult, A.add)
    op("v", [], "ts", col(15), col(LF), 14.0, None, A.not_equal)
    op("v", [], "ts", col(16), col(LF), 10.0, None, A.not_equal)
    op("v", [], "ts", col(17), col(LF), 14.0, None, A.is_equal)
    k4 = op("v", [], "ts", col(18), col(LF), 10.0, 17.0, A.is_equal, A.mult)
    op("v", [k4], "tt", col(19), col(15), col(16), A.mult)
    k5 = op("v", [], "tt", col(20), col(17), col(18), A.add)
    k6 = op("v", [k5, gi3], "ts", cf[:, 32:40], ci[:, 32:40], col(19), col(20), A.mult, A.add)
    k7 = op("v", [], "tt", col(21), col(GF), col(14), A.mult)
    v_ul = op("v", [k6], "cp", T.uls[:], cf[:, 32:40])
    k8 = op("v", [k7], "ts", col(22), col(21), 1.0 - 2.0 ** -15, 2.0 ** -15, A.mult, A.add)
    g_eb = op("g", [v_one], "sel", T.eb[:], T.one[:], [[-1, 516]], A.is_equal, 0.0, 3, 4)
    g_iw = op("g", [], "iota", T.iw[:], [[1, 320]], 0, 0, allow_small_or_imprecise_dtypes=True)
    v64 = op("s", [g_eb], "act", T.eb64[:], T.eb[:], AF.Copy, scale=64.0)
    op("v", [], "ms", T.kx[:, 0:120 * R:2], 4680.0 * 2.0 ** -15)
    op("v", [], "ms", T.kx[:, 1:120 * R:2], 4680.0)
    op("v", [], "ms", T.hb[:], 1)
    g1 = op("v", [], "ms", T.sg[:], 1.0)
    seg = op("v", [g1], "ms", T.sg[:, 0:100:5], 0.0)
    k9 = op("v", [q2, k8], "ts", col(23), col(10), MAGIC, col(22), A.subtract, A.mult)
    nt, ni, nf, tw = T.nt, T.ni, T.nf, T.tw
    w1 = op("v", [done("ld_nx"), gn], "ts", nf[:, 0:640], nt[:], -159.5, BIG, A.add, A.add)
    w2 = op("s", [w1], "act", nf[:, 640:1280], nf[:, 0:640], AF.Identity, bias=-BIG)
    w3 = op("s", [w2, c5], "act", nf[:, 1280:1920], nf[:, 640:1280], AF.Exp, bias=col(13), scale=col(12))
    w4 = op("s", [w3], "act", nf[:, 1920:2560], nf[:, 1280:1920], AF.Identity, bias=MAGIC)
    op("v", [k9], "tt", col(24), col(23), col(YF), A.mult)
    c8 = op("v", [], "tt", col(25), col(23), col(14), A.mult)
    qu = op("v", [("ld_u", 16)], "qz", T.uq[:], T.up[:], T.ub[:])
    op("v", [qu, v_ul], "cp", T.uq2[:].bitcast(dt.uint32), T.uq[:].bitcast(dt.uint32).indirect(T.uls[:]))
    v_u = op("v", [], "cp", T.up2[:], T.up[:].indirect(T.uls[:]))
    qx = [op("v", [("ld_x%d" % h, 16)], "qz", T.qx0[:, H * h:H * h + H], T.sx0[:, H * h:H * h + H], T.x0[:, 640 * h:640 * h + 640])
          for h in range(2)]

    def send_codes(r, h, tok):
        need("g", [tok])
        es = topo.engines(core, rel[1])
        n = len(es) // 2
        tr = []
        for k in (1, 2):
            a = H * h + 80 * (k - 1)
            rid, pid = topo.addr(rel[k], core)
            tr.append(RemoteDMATransfer(dst_ids=[DstId(rid=rid, pnc=pid)], dma_engine_mask=_mask(es[n * k - n:n * k]),
                                        remote_sem=T.sem["rc%d%d" % (r, h)], src=T["qx%d" % r][:, a:a + 80].bitcast(dt.uint8),
                                        dst=T["rq%d" % r][:, a:a + 80].bitcast(dt.uint8)))
        g.remote_dma_fused(tr, local_sem=T.sem.loc)
        rid, pid = topo.addr(rel[0], core)
        g.remote_dma(T["rs%d" % r][:, H * h:H * h + H], T["sx%d" % r][:, H * h:H * h + H], T.sem["rp%d%d" % (r, h)],
                     T.sem.loc, pid, rid, topo.mask(core, rel[0]))
        loc[0] += 4 * n

    def scores(r, h, tok):
        k = bank()
        return k, mm([tok, v_u], k, H, T.uq2, T.up2, 0, T["qx%d" % r], T["sx%d" % r], H * h)

    def bits(r, h, kt):
        k, t = kt
        o = op("v", [t], "ts", T["bw%d" % r][:, H * h:H * h + H], banks[k][:, 0:H], 0.0, None, A.is_gt)
        readers[k].append(o)
        return o

    def unpack(r, h, tok, own=True):
        ps = []
        for b in range(4):
            k = bank()
            qc, qs = (T["qx%d" % r], T["sx%d" % r]) if own else (T["qp%d" % r], T["sp%d" % r])
            ps.append((k, mm([tok, vE], k, H, T.ec, T.es, b, qc, qs, H * h)))
        return ps

    def unpack_copy(r, h, ps, own=True):
        d = T["f%d" % r] if own else T["fp%d" % r]
        for b in range(4):
            k, t = ps[b]
            o = op("s", [t], "act", d[:, 320 * b + H * h:320 * b + H * h + H], banks[k][:, 0:H], AF.Copy)
            readers[k].append(o)
        return o

    def edge_rows(r, h, tok):
        return op("s", [tok, v_id], "act", T["er%d" % r][:, 320 * h:320 * h + 320],
                  T["bw%d" % r][:, H * h:H * h + H].indirect(T.idl[:]), AF.Copy)

    sc = [scores(0, 0, qx[0]), scores(0, 1, qx[1])]
    send_codes(0, 0, qx[0])
    send_codes(0, 1, qx[1])
    i1 = op("v", [g_id], "ts", ci[:, 40:60], ni[:, 0:20], col(LF), None, A.add)
    n1 = op("v", [i1], "ts", ni[:], nt[:], 511, None, A.bitwise_and)
    v_id = op("v", [i1], "cp", T.idl[:], ci[:, 40:60])
    n2 = op("v", [n1], "tt", nf[:, 2560:2880], ni[:, 0:320], ni[:, 320:640], A.subtract)
    w5 = op("v", [w4], "tt", nf[:, 3200:3520], nf[:, 1920:2240], nf[:, 2240:2560], A.subtract)
    bt_ = [bits(0, 0, sc[0]), bits(0, 1, sc[1])]
    n3 = op("s", [n2, c8], "act", nf[:, 2880:3200], nf[:, 2560:2880], AF.Copy, scale=col(24))
    w6 = op("s", [w5, c8], "act", nf[:, 3520:3840], nf[:, 3200:3520], AF.Copy, scale=col(25))
    l0 = T.l0
    op("v", [], "ts", col(26), col(GF), -320.0, 320.0, A.mult, A.add)
    c2 = op("v", [], "ts", col(27), col(GF), 320.0, None, A.mult)
    v_l0 = op("v", [("ld_al", 16)], "cp", l0[:], T.ali[:])

    def dup(dst, src, toks, h):
        a = 20 * h
        op("v", [toks, c2], "cp", dst[:, 20 + a:40 + a:2], src)
        op("v", [], "cp", dst[:, 21 + a:40 + a:2], src)
        op("v", [], "ts", dst[:, 60 + a:80 + a:2], src, col(27), None, A.add)
        return op("v", [], "ts", dst[:, 61 + a:80 + a:2], src, col(26), None, A.add)
    lists = [dup(T.us0, l0[:, 10 * h:10 * h + 10], [v_l0], h) for h in range(2)]
    c3 = op("v", [], "ts", col(11), col(GF), -4680.0 * 2.0 ** -15, 4680.0 * 2.0 ** -15, A.mult, A.add)
    for q in range(4):
        wl = op("v", [w6, n3], "tt", tw[:, q:320:4], nf[:, 2880 + 80 * q:2960 + 80 * q], nf[:, 3520 + 80 * q:3600 + 80 * q], A.add)
    v_tw = op("s", [wl, k1], "act", tw[:, 320:640], tw[:, 0:320], AF.Copy, scale=col(14))
    for b in range(4):
        vE = op("v", [g_eb], "qz", T.ec[:, 128 * b:128 * b + 128], T.es[:, 128 * b:128 * b + 128], T.eb[:, 3 - b:515 - b])
    pF = unpack(0, 0, qx[0])
    tF = [None, None]

    def table_lookup(r, h, e, tok):
        out, win = T["tr%d" % r][:, 320 * h:320 * h + 320], tw[:].indirect(T["us%d" % r][:, 60 + 20 * h:80 + 20 * h])
        return op("v", [tok, v_tw], "cp", out, win) if e == "v" else op("s", [tok, v_tw], "act", out, win, AF.Copy)

    def table_turn(r, h, tok):
        a, gt, fs = 320 * h, T["gt%d" % r], T["fs%d" % r]
        t = op("v", [tok], "tp", gt[:, a:a + 320], T["tr%d" % r][:, a:a + 320])
        x1, x2 = fs[:, 80 + 40 * h:120 + 40 * h], fs[:, 920 + 40 * h:960 + 40 * h]
        op("v", [t], "tt", x1, gt[:, a:a + 320:8], gt[:, a + 2:a + 320:8], A.add)
        p = op("v", [], "tt", x2, gt[:, a + 4:a + 320:8], gt[:, a + 6:a + 320:8], A.add)
        return op("v", [p], "tt", fs[:, 40 * h:40 * h + 40], x1, x2, A.add)

    trow = [table_lookup(0, 0, "s", lists[0]), table_lookup(0, 1, "v", lists[1])]
    for r in range(R):
        rn = r + 1
        us, fs, ints, bw = T["us%d" % r], T["fs%d" % r], T["is%d" % r], T["bw%d" % r]
        br, btb, gt = T["br%d" % r], T["bt%d" % r], T["gt%d" % r]
        kb, hh = 120 * r, 100 * r
        cur = (l0[:, 0:10], l0[:, 10:20]) if r == 0 else (T["us%d" % (r - 1)][:, 0:10], T["ll%d" % (r - 1)][:])
        p1 = op("v", [bt_, lists], "cp", br[:, 0:320], bw[:].indirect(us[:, 20:40]))
        p2 = op("s", [bt_, lists], "act", br[:, 320:640], bw[:].indirect(us[:, 40:60]), AF.Copy)
        if r == 0:
            er = [edge_rows(0, 0, bt_[0]), None]
            tab = [table_turn(0, h, trow[h]) for h in range(2)]
        er[1] = edge_rows(r, 1, bt_[1])
        v_bt = op("v", [p1, p2], "tp", btb[:], br[:])
        km = op("v", [v_bt, tab], "tt", fs[:, 160:200], fs[:, 1:80:2], btb[:, 0:640:16], A.mult)
        ks = op("v", [km], "tt", fs[:, 200:240], fs[:, 160:200], fs[:, 0:80:2], A.add)
        for d in (1, 2, 3):
            dma("y", [ks], T.kx[32 * d:128, kb + 40 * (3 - d):kb + 40 * (4 - d)], fs[0:128 - 32 * d, 200:240], "kx%d" % r)
        if r == 0:
            tF[0] = unpack_copy(0, 0, pF)
        tF[1] = unpack_copy(r, 1, unpack(r, 1, qx[1]))
        nm = [op("v", [v_bt], "tt", fs[:, 240 + 40 * e:280 + 40 * e], gt[:, 9 + 2 * e:640:16], btb[:, 0:640:16], A.mult) for e in range(4)]
        ko = op("v", [ks, c3], "ts", fs[:, 860:880], fs[:, 200:240:2], col(GF), col(11), A.mult, A.add)
        ns = [op("v", [nm[e]], "tt", fs[:, 400 + 40 * e:440 + 40 * e], fs[:, 240 + 40 * e:280 + 40 * e], gt[:, 1 + 2 * e:640:16], A.add)
              for e in range(4)]
        op("v", [], "cp", fs[:, 560:610:5], cur[0])
        op("v", [], "cp", fs[:, 610:660:5], cur[1])
        et = T["et%d" % r]
        e1 = op("v", [er], "tp", et[:], T["er%d" % r][:])
        de = [op("v", [ns[e]], "tt", fs[:, 561 + e:660:5], fs[:, 400 + 40 * e:440 + 40 * e:2], fs[:, 401 + 40 * e:440 + 40 * e:2], A.add)
              for e in range(4)]
        op("v", [e1], "ts", fs[:, 880:900], et[:, 14:640:32], 3.0, 1.0, A.mult, A.add)
        e3 = op("v", [], "ts", fs[:, 900:920], et[:, 10:640:32], 32768.0, 32768.0, A.mult, A.add)
        st = op("v", [e3], "tt", ints[:, 0:20], fs[:, 880:900], fs[:, 900:920], A.mult)
        sv, at = ints[:, 0:20], 20
        for j in range(6):
            tv = ints[:, at:at + 20]
            a = kb + 40 * (j // 2) + j % 2
            st = op("v", [st, done("kx%d" % r)], "tt", tv, T.kx[:, a:kb + 40 * (j // 2) + 40:2], sv, A.mult)
            sv = ints[:, at + 20:at + 40]
            st = op("v", [st], "ts", sv, tv, 0x78000 if j % 2 else 0x8888, None, A.bitwise_and)
            at += 40
        tv = ints[:, at:at + 20]
        st = op("v", [st, ko], "tt", tv, fs[:, 860:880], sv, A.mult)
        hs = [op("v", [st], "ts", T.hb[:, hh + 1 + e:hh + 100:5], tv, 1 << (4 * e + 3), None, A.bitwise_and) for e in range(4)]
        st = op("v", [hs, de], "tt", fs[:, 660:760], T.hb[:, hh:hh + 100], fs[:, 560:660], A.mult)
        st = op("v", [st, seg], "scan", fs[:, 760:860], T.sg[:], fs[:, 660:760], 0.0, A.mult, A.add)
        lm = op("v", [st], "cp", us[:, 10:20], fs[:, 814:860:5])
        need("g", [lm])
        rid, pid = topo.addr(rel[0], core)
        g.remote_dma(T["rl%d" % r][:], us[:, 10:20], T.sem["rl%d" % r], T.sem.loc, pid, rid, topo.mask(core, rel[0]))
        loc[0] += len(topo.engines(core, rel[0]))
        ls = op("v", [], "cp", us[:, 0:10], fs[:, 764:810:5])
        qa = [("qa%d%d" % (r, h), 3 * far_engines) for h in range(2)]
        tP = [unpack_copy(r, 0, unpack(r, 0, qa[0], own=False), own=False), None]
        if r == 0:
            for b in range(4):
                v64q = op("v", [v64], "qz", T.e64c[:, 128 * b:128 * b + 128], T.e64s[:, 128 * b:128 * b + 128], T.eb64[:, 3 - b:515 - b])

        def make(h, toks, off, F):
            z, q, s, o = T["z%d" % r], T["qz%d" % r], T["sz%d" % r], []
            for b in range(4):
                win, out = F[:, 320 * b:320 * b + 320].indirect(off), z[:, 640 * h + b:640 * h + 640:4]
                o.append(op("v", [toks], "cp", out, win) if b < 2 else op("s", [toks], "act", out, win, AF.Copy))
            zq = op("v", [o], "qz", q[:, H * h:H * h + H], s[:, H * h:H * h + H], z[:, 640 * h:640 * h + 640])
            ps = []
            for b in range(4):
                k = bank()
                mm([zq, ("ld_w", 32)], k, H, T.wq, T.wp, b, q, s, H * h, True, False)
                ps.append((k, mm([zq, v64q], k, H, T.e64c, T.e64s, b, q, s, H * h, False, True)))
            return ps

        def renew(h, b, ps, e):
            k, t = ps[b]
            out = T["x%d" % rn][:, 640 * h + b:640 * h + 640:4]
            o = op("v", [t], "ts", out, banks[k][:, 0:H], 0.015625, None, A.mult) if e == "v" else \
                op("s", [t], "act", out, banks[k][:, 0:H], AF.Copy, scale=0.015625)
            readers[k].append(o)
            return o

        def requant(h, toks):
            return op("v", [toks], "qz", T["qx%d" % rn][:, H * h:H * h + H], T["sx%d" % rn][:, H * h:H * h + H],
                      T["x%d" % rn][:, 640 * h:640 * h + 640])

        def outputs(h, tok, ea, eb):
            k = bank()
            t = mm([tok, vv], k, H, T.vq, T.vp, 0, T["qx%d" % rn], T["sx%d" % rn], H * h)
            dma(ea, [tok], T.oc[:, 640 * h:640 * h + 640], T["qx%d" % rn][:, H * h:H * h + H].bitcast(dt.uint8), "outs")
            for i in range(4):
                dma(eb if i % 2 else ea, [tok], T.osc[4 * i:4 * i + 4, H * h:H * h + H], T["sx%d" % rn][32 * i:32 * i + 4, H * h:H * h + H], "outs")
            o = op("v", [t], "cp", T.yb[:, H * h:H * h + H], banks[k][:, 0:H])
            readers[k].append(o)
            dma(ea, [o], T.y[:, H * h:H * h + H], T.yb[:, H * h:H * h + H], "outs")

        ps = make(0, [ls, tF], us[:, 0:10], T["f%d" % r])
        if rn < R:
            lists = [dup(T["us%d" % rn], us[:, 0:10], [ls], 0), None]
        else:
            vv = op("v", [("ld_v", 16)], "qz", T.vq[:], T.vp[:], T.vb[:])
        o = [renew(0, b, ps, "v" if b % 2 else "s") for b in range(4)]
        tP[1] = unpack_copy(r, 1, unpack(r, 1, qa[1], own=False), own=False)
        qx = [requant(0, o), None]
        land, la = T["ll%d" % r], ("la%d" % r, far_engines)
        if rn < R:
            s0 = scores(rn, 0, qx[0])
            p0 = unpack(rn, 0, qx[0])
            send_codes(rn, 0, qx[0])
            t0 = table_lookup(rn, 0, "s", lists[0])
            tF = [unpack_copy(rn, 0, p0), None]
            bt_ = [bits(rn, 0, s0), None]
            tab = [table_turn(rn, 0, t0), None]
            er = [edge_rows(rn, 0, bt_[0]), None]
        else:
            oa1 = op("s", [ls, g_iw], "act", T.orow[:, 0:H], T.iw[:].indirect(us[:, 0:10]), AF.Copy)
            outputs(0, qx[0], "y", "y")
        ps = make(1, [la, tP], land[:], T["fp%d" % r])
        if rn < R:
            lists[1] = dup(T["us%d" % rn], land[:], [la], 1)
            tab[1] = table_turn(rn, 1, table_lookup(rn, 1, "v", lists[1]))
        else:
            oa2 = op("v", [la, g_iw], "cp", T.orow[:, H:C], T.iw[:].indirect(land[:]))
            dma("y", [oa1, oa2], T.oa[:], T.orow[0:128:16, :], "outs")
        o = [renew(1, b, ps, "s") for b in range(4)]
        qx[1] = requant(1, o)
        if rn < R:
            send_codes(rn, 1, qx[1])
            bt_[1] = bits(rn, 1, scores(rn, 1, qx[1]))
        else:
            outputs(1, qx[1], "y", "s")
    need("g", [("loc", loc[0]), done("outs")])
    for e in ("v", "s", "t", "g"):
        need("g", [(e + "q", cnt[e])])
